import numpy as np
import ml_dtypes


def mxq(x, axis, fmt="e4m3"):
    dtype, down = {"e4m3": (ml_dtypes.float8_e4m3fn, 7), "e5m2": (ml_dtypes.float8_e5m2, 14)}[fmt]
    v = np.moveaxis(np.asarray(x, np.float32).astype(ml_dtypes.bfloat16).astype(np.float64), axis, -1)
    blocks = v.reshape(v.shape[:-1] + (-1, 32))
    amax = np.abs(blocks).max(-1, keepdims=True)
    byte = np.maximum(np.where(amax > 0, np.frexp(amax)[1] - 1 + 127, 0) - down, 1)
    scale = np.exp2(byte - 127.0)
    codes = (blocks / scale).astype(np.float32).astype(dtype).astype(np.float64)
    return np.moveaxis((codes * scale).reshape(v.shape), -1, axis)


WIDE = False


def mx_kscale(k):
    if not WIDE:
        return np.ones(k)
    levels = np.array([10, -10, 5, -5, 0])
    if k % 512:
        return np.exp2(np.random.permutation(np.resize(levels, k // 32))).repeat(32)
    a = np.empty((k // 512, 16))
    for p in range(k // 512):
        a[p, :8] = np.random.permutation(np.resize(levels, 8))
        for g in range(8):
            far = levels[np.abs(levels - a[p, g]) >= 10]
            a[p, g + 8] = far[np.random.randint(len(far))]
    return np.exp2(a.ravel()).repeat(32)


def f64(x):
    return np.asarray(x).astype(np.float64)


def striped(idx):
    return np.tile(idx.reshape(-1, 16).T, (8, 1)).astype(np.uint16)


def unstriped(offs):
    return offs[:16].T.reshape(-1).astype(np.int64)


def relu2(v):
    return np.maximum(v, 0.0) ** 2


K, T, D, S, V, N = 1024, 2048, 4, 512, 256, 512


def setup_inputs():
    n = np.random.standard_normal
    s = mx_kscale(K)[:, None]
    return {
        "xT": (n((K, T)) * s).astype(np.float32),
        "w": (n((K, N)) / np.sqrt(K) / s).astype(np.float32),
        "b": (0.3 * n((N, 1))).astype(np.float32),
        "gate": np.tile(np.random.uniform(0.2, 1.0, (D, 1, V)) / np.sqrt(D), (1, N, 1)).astype(np.float32),
        "offs": striped(np.random.permutation(T)[:S]),
        "pos1": striped(np.random.permutation(S)[:V]),
        "pos2": striped(np.random.permutation(S)[:V]),
        "pos3": striped(np.random.permutation(S)[:V]),
        "pos4": striped(np.random.permutation(S)[:V]),
    }


def reference(xT, w, b, gate, offs, pos1, pos2, pos3, pos4):
    idx = unstriped(offs)
    xq = mxq(f64(xT)[:, idx], 0, "e4m3")
    y = mxq(f64(w), 0, "e4m3").T @ xq
    y = relu2(y + f64(b))
    return sum(f64(gate[d]) * y[:, unstriped(p)] for d, p in enumerate((pos1, pos2, pos3, pos4)))

@@ -1,0 +1,231 @@
+from contextlib import ExitStack
+
+import concourse.mybir as mybir
+from concourse.masks import make_identity
+
+K, T, D, S, V, N = 1024, 2048, 4, 512, 256, 512
+FLOPS = 2 * K * N * S
+
+F32 = mybir.dt.float32
+BF16 = mybir.dt.bfloat16
+U32 = mybir.dt.uint32
+U16 = mybir.dt.uint16
+U8 = mybir.dt.uint8
+FP8X4 = mybir.dt.float8_e4m3fn_x4
+ACT = mybir.ActivationFunctionType
+ALU = mybir.AluOpType
+
+P = 128
+PACK = 4
+K_PASS = P * PACK
+PASSES = K // K_PASS
+BLOCKS = N // P
+HALF = S // 2
+LIST_ROWS = 16
+
+
+def tile_picked_sub_lin_relu2_sub_e_kernel(tc, xT, w, b, gate, offs, pos1, pos2, pos3, pos4, out):
+    nc = tc.nc
+    with ExitStack() as ctx:
+        keep = ctx.enter_context(tc.tile_pool(name="keep", bufs=1))
+        psum = ctx.enter_context(tc.psum_pool(name="psum", bufs=1))
+
+        def sbuf(name, shape, dtype, after=None):
+            return keep.tile(shape, dtype, name=name, tag=after or name, align_bytes=64)
+
+        offs_sb = keep.tile([P, S // LIST_ROWS], U16, name="offs_sb")
+        pos_sb = [keep.tile([P, V // LIST_ROWS], U16, name=f"pos_sb{d}") for d in range(D)]
+        x_raw = [[sbuf(f"x_raw{a}{j}", [P, T], F32) for j in range(PACK)] for a in range(PASSES)]
+        w_raw = [[sbuf(f"w_raw{a}{h}", [P, PACK, 2 * P], F32) for h in range(2)] for a in range(PASSES)]
+        gate_first = [sbuf(f"gate_first{u}", [P, 2, V], F32) for u in range(2)]
+        gate_sb = [None] + [sbuf(f"gate_sb{c}", [P, D, V], F32) for c in range(1, BLOCKS)]
+        x_bf = [sbuf(f"x_bf{a}", [P, S, PACK], BF16) for a in range(PASSES)]
+        x_codes = [sbuf(f"x_codes{a}", [P, S], U32) for a in range(PASSES)]
+        x_scales = [sbuf(f"x_scales{a}", [P, S], U8) for a in range(PASSES)]
+        y = [sbuf(f"y{c}", [P, S], F32) for c in range(BLOCKS)]
+        result = [sbuf(f"result{c}", [P, V], F32) for c in range(BLOCKS)]
+        ident = sbuf("ident", [P, P], F32)
+        bias_rows = sbuf("bias_rows", [P, P], F32)
+        bias = sbuf("bias", [P, BLOCKS], F32)
+        warm = sbuf("warm", [P, 2], F32)
+        w_bf, w_codes, w_scales, prod = {}, {}, {}, {}
+
+        z_first = [psum.tile([P, HALF], F32, name=f"z_first{u}", tag=f"pair{u}") for u in range(2)]
+        z = [None] + [psum.tile([P, S], F32, name=f"z{c}", tag=f"z{c}") for c in range(1, BLOCKS)]
+
+        x_rows = xT.rearrange("(a p j) t -> a j p t", a=PASSES, j=PACK)
+        w_rows = w.rearrange("(a p j) (h m) -> a h p j m", a=PASSES, j=PACK, h=2)
+        gate_rows = gate.rearrange("d (c p) v -> c p d v", p=P)
+
+        def load_x(a, j):
+            nc.sync.dma_start(x_raw[a][j][:], x_rows[a, j])
+
+        def load_w(a, h):
+            nc.sync.dma_start(w_raw[a][h][:], w_rows[a, h])
+
+        load_x(0, 0)
+        nc.sync.dma_start(offs_sb[:], offs)
+        load_x(0, 1)
+        load_w(0, 0)
+        load_w(1, 0)
+        load_x(0, 2)
+        load_x(0, 3)
+        for j in range(PACK):
+            load_x(1, j)
+        load_w(0, 1)
+        load_w(1, 1)
+        for d, pos in enumerate((pos1, pos2, pos3, pos4)):
+            nc.sync.dma_start(pos_sb[d][:], pos)
+        for u in range(2):
+            nc.sync.dma_start(gate_first[u][:], gate_rows[0, :, 2 * u : 2 * u + 2, :])
+        for c in range(1, BLOCKS):
+            nc.sync.dma_start(gate_sb[c][:], gate_rows[c])
+
+        nc.vector.memset(bias_rows[:], 0.0)
+        nc.scalar.dma_start(bias_rows[0:BLOCKS, :], b.rearrange("(c p) o -> c (p o)", p=P))
+        make_identity(nc, ident[:])
+        nc.scalar.activation(warm[:, 0:1], ident[:, 0:1], ACT.Relu)
+        nc.scalar.activation(warm[:, 1:2], ident[:, 0:1], ACT.Square)
+        bias_ps = psum.tile([P, P], F32, name="bias_ps", tag="back", bufs=2)
+        nc.tensor.transpose(bias_ps[:], bias_rows[:], ident[:])
+        nc.scalar.copy(bias[:], bias_ps[:, 0:BLOCKS])
+
+        def gather_x(a, j, lo, hi):
+            window = x_raw[a][j][:].indirect(offs_sb[:, lo // LIST_ROWS : hi // LIST_ROWS])
+            nc.vector.tensor_copy(x_bf[a][:, lo:hi, j], window)
+
+        def quantize_x(a, lo, hi):
+            nc.vector.quantize_mx(
+                out=x_codes[a][:, lo:hi].bitcast(FP8X4),
+                scales=x_scales[a][:, lo:hi],
+                in_=x_bf[a][:, lo:hi, :].rearrange("p s j -> p (s j)"),
+            )
+
+        def interleave_w(copy, a, first, count, after=None):
+            w_bf[a, first] = sbuf(f"w_bf{a}{first}", [P, count * P, PACK], BF16, after)
+            cols = slice((first % 2) * P, (first % 2 + count) * P)
+            copy(w_bf[a, first][:], w_raw[a][first // 2][:, :, cols].rearrange("p j m -> p m j"))
+
+        def quantize_w(a, first, count, after=None):
+            codes = sbuf(f"w_codes{a}{first}", [P, count * P], U32, after)
+            scales = sbuf(f"w_scales{a}{first}", [P, count * P], U8)
+            nc.vector.quantize_mx(out=codes[:].bitcast(FP8X4), scales=scales[:], in_=w_bf[a, first][:].rearrange("p m j -> p (m j)"))
+            for i in range(count):
+                w_codes[a, first + i] = codes[:, i * P : (i + 1) * P]
+                w_scales[a, first + i] = scales[:, i * P : (i + 1) * P]
+
+        def product(acc, a, c, lo, hi):
+            nc.tensor.matmul_mx(
+                out=acc,
+                lhsT=w_codes[a, c].bitcast(FP8X4),
+                lhsT_scale=w_scales[a, c],
+                rhs=x_codes[a][:, lo:hi].bitcast(FP8X4),
+                rhs_scale=x_scales[a][:, lo:hi],
+                start=(a == 0),
+                stop=(a == PASSES - 1),
+            )
+
+        def activate(c):
+            relu = sbuf(f"relu{c}", [P, S], F32)
+            nc.scalar.activation(relu[:], z[c][:], ACT.Relu, bias=bias[:, c : c + 1])
+            nc.scalar.activation(y[c][:], relu[:], ACT.Square)
+
+        def neighbour(c, d, after=None):
+            prod[c, d] = sbuf(f"prod{c}{d}", [P, V], F32, after)
+            weights = gate_first[d // 2][:, d % 2, :] if c == 0 else gate_sb[c][:, d, :]
+            nc.vector.tensor_tensor(prod[c, d][:], y[c][:].indirect(pos_sb[d][:]), weights, ALU.mult)
+
+        def turn_and_add(acc, c, d, u, count):
+            nc.tensor.matmul(
+                acc, prod[c, d][:, u * P : (u + 1) * P], ident[:], start=(d == 0), stop=(d == count - 1), is_transpose=True
+            )
+
+        def turn_back(c, turned_sb):
+            back = psum.tile([P, V], F32, name=f"back{c}", tag="back", bufs=2)
+            for u in range(2):
+                nc.tensor.transpose(back[:, u * P : (u + 1) * P], turned_sb[:, u, :], ident[:])
+            return back
+
+        def store(c):
+            nc.sync.dma_start(out[c * P : (c + 1) * P, :], result[c][:])
+
+        def sum_whole(c, tag):
+            turned = psum.tile([P, 2, P], F32, name=f"turned{c}", tag=tag)
+            for u in range(2):
+                for d in range(D):
+                    turn_and_add(turned[:, u, :], c, d, u, D)
+            turned_sb = sbuf(f"turned_sb{c}", [P, 2, P], F32)
+            nc.scalar.copy(turned_sb[:], turned[:])
+            nc.scalar.copy(result[c][:], turn_back(c, turned_sb)[:])
+            store(c)
+
+        def sum_part(c, tags):
+            turned = [psum.tile([P, P], F32, name=f"turned{c}{u}", tag=tags[u]) for u in range(2)]
+            for d in range(D - 1):
+                for u in range(2):
+                    turn_and_add(turned[u][:], c, d, u, D - 1)
+            turned_sb = sbuf(f"turned_sb{c}", [P, 2, P], F32)
+            for u in range(2):
+                nc.scalar.copy(turned_sb[:, u, :], turned[u][:])
+            return turn_back(c, turned_sb)
+
+        gather_x(0, 0, 0, S)
+        gather_x(0, 1, 0, S)
+        for a in range(PASSES):
+            interleave_w(nc.scalar.copy, a, 0, 2)
+        gather_x(0, 2, 0, S)
+        for a in range(PASSES):
+            quantize_w(a, 0, 2)
+        gather_x(0, 3, 0, S)
+        quantize_x(0, 0, S)
+        for u in range(2):
+            product(z_first[u][:], 0, 0, u * HALF, (u + 1) * HALF)
+        product(z[1][:], 0, 1, 0, S)
+        for j in range(PACK - 1):
+            gather_x(1, j, 0, S)
+        for u in range(2):
+            gather_x(1, PACK - 1, u * HALF, (u + 1) * HALF)
+        for u in range(2):
+            quantize_x(1, u * HALF, (u + 1) * HALF)
+            product(z_first[u][:], 1, 0, u * HALF, (u + 1) * HALF)
+        product(z[1][:], 1, 1, 0, S)
+        relu_first = [sbuf(f"relu_first{u}", [P, HALF], F32) for u in range(2)]
+        for u in range(2):
+            nc.scalar.activation(relu_first[u][:], z_first[u][:], ACT.Relu, bias=bias[:, 0:1])
+        for c in (2, 3):
+            interleave_w(nc.vector.tensor_copy, 0, c, 1)
+        for c in (2, 3):
+            quantize_w(0, c, 1)
+        for u in range(2):
+            nc.vector.tensor_tensor(y[0][:, u * HALF : (u + 1) * HALF], relu_first[u][:], relu_first[u][:], ALU.mult)
+        product(z[2][:], 0, 2, 0, S)
+        product(z[3][:], 0, 3, 0, S)
+        activate(1)
+        interleave_w(nc.scalar.copy, 1, 2, 1, after="relu_first0")
+        interleave_w(nc.scalar.copy, 1, 3, 1, after="relu_first1")
+        for d in range(2):
+            neighbour(0, d)
+        quantize_w(1, 2, 1, after="gate_first0")
+        product(z[2][:], 1, 2, 0, S)
+        for d in range(2, D):
+            neighbour(0, d)
+        quantize_w(1, 3, 1, after="gate_first1")
+        product(z[3][:], 1, 3, 0, S)
+        activate(2)
+        neighbour(1, 0, after="relu_first0")
+        neighbour(1, 1)
+        neighbour(1, 2, after="relu_first1")
+        neighbour(1, 3)
+        activate(3)
+        sum_whole(0, "z2")
+        sum_whole(1, "z3")
+        backs = {}
+        for c, tags in ((2, ("pair0", "pair1")), (3, ("z1", "spare"))):
+            for d in range(D - 1):
+                neighbour(c, d)
+            backs[c] = sum_part(c, tags)
+        for c in (2, 3):
+            neighbour(c, D - 1)
+        for c in (2, 3):
+            nc.vector.tensor_tensor(result[c][:], prod[c, D - 1][:], backs[c][:], ALU.add)
+            store(c)

@@ -36,9 +36,6 @@ def tile_picked_sub_lin_relu2_sub_e_kernel(tc, xT, w, b, gate, offs, pos1, pos2,
         offs_sb = keep.tile([P, S // LIST_ROWS], U16, name="offs_sb")
         pos_sb = [keep.tile([P, V // LIST_ROWS], U16, name=f"pos_sb{d}") for d in range(D)]
         x_raw = [[sbuf(f"x_raw{a}{j}", [P, T], F32) for j in range(PACK)] for a in range(PASSES)]
-        w_raw = [[sbuf(f"w_raw{a}{h}", [P, PACK, 2 * P], F32) for h in range(2)] for a in range(PASSES)]
-        gate_first = [sbuf(f"gate_first{u}", [P, 2, V], F32) for u in range(2)]
-        gate_sb = [None] + [sbuf(f"gate_sb{c}", [P, D, V], F32) for c in range(1, BLOCKS)]
         x_bf = [sbuf(f"x_bf{a}", [P, S, PACK], BF16) for a in range(PASSES)]
         x_codes = [sbuf(f"x_codes{a}", [P, S], U32) for a in range(PASSES)]
         x_scales = [sbuf(f"x_scales{a}", [P, S], U8) for a in range(PASSES)]
@@ -48,38 +45,52 @@ def tile_picked_sub_lin_relu2_sub_e_kernel(tc, xT, w, b, gate, offs, pos1, pos2,
         bias_rows = sbuf("bias_rows", [P, P], F32)
         bias = sbuf("bias", [P, BLOCKS], F32)
         warm = sbuf("warm", [P, 2], F32)
-        w_bf, w_codes, w_scales, prod = {}, {}, {}, {}
+        w_raw, w_bf, w_codes, w_scales, gate_sb, prod = {}, {}, {}, {}, {}, {}
 
         z_first = [psum.tile([P, HALF], F32, name=f"z_first{u}", tag=f"pair{u}") for u in range(2)]
         z = [None] + [psum.tile([P, S], F32, name=f"z{c}", tag=f"z{c}") for c in range(1, BLOCKS)]
 
         x_rows = xT.rearrange("(a p j) t -> a j p t", a=PASSES, j=PACK)
-        w_rows = w.rearrange("(a p j) (h m) -> a h p j m", a=PASSES, j=PACK, h=2)
+        w_rows = w.rearrange("(a p j) m -> a p j m", a=PASSES, j=PACK)
         gate_rows = gate.rearrange("d (c p) v -> c p d v", p=P)
 
         def load_x(a, j):
             nc.sync.dma_start(x_raw[a][j][:], x_rows[a, j])
 
-        def load_w(a, h):
-            nc.sync.dma_start(w_raw[a][h][:], w_rows[a, h])
+        def load_w(a, first, count):
+            raw = sbuf(f"w_raw{a}{first}", [P, PACK, count * P], F32)
+            nc.sync.dma_start(raw[:], w_rows[a, :, :, first * P : (first + count) * P])
+            for i in range(count):
+                w_raw[a, first + i] = raw[:, :, i * P : (i + 1) * P]
+
+        def load_gate(c, first, count):
+            tile = sbuf(f"gate{c}{first}", [P, count, V], F32)
+            nc.sync.dma_start(tile[:], gate_rows[c, :, first : first + count, :])
+            for i in range(count):
+                gate_sb[c, first + i] = tile[:, i, :]
 
         load_x(0, 0)
         nc.sync.dma_start(offs_sb[:], offs)
+        for d, pos in enumerate((pos1, pos2, pos3, pos4)):
+            nc.sync.dma_start(pos_sb[d][:], pos)
         load_x(0, 1)
-        load_w(0, 0)
-        load_w(1, 0)
+        load_w(0, 0, 2)
         load_x(0, 2)
         load_x(0, 3)
         for j in range(PACK):
             load_x(1, j)
-        load_w(0, 1)
-        load_w(1, 1)
-        for d, pos in enumerate((pos1, pos2, pos3, pos4)):
-            nc.sync.dma_start(pos_sb[d][:], pos)
-        for u in range(2):
-            nc.sync.dma_start(gate_first[u][:], gate_rows[0, :, 2 * u : 2 * u + 2, :])
-        for c in range(1, BLOCKS):
-            nc.sync.dma_start(gate_sb[c][:], gate_rows[c])
+        load_w(1, 0, 1)
+        load_w(1, 1, 1)
+        load_w(0, 2, 2)
+        load_gate(0, 0, 2)
+        load_gate(0, 2, 2)
+        load_w(1, 2, 1)
+        load_gate(1, 0, 2)
+        load_w(1, 3, 1)
+        load_gate(1, 2, 2)
+        load_gate(2, 0, D)
+        load_gate(3, 0, D - 1)
+        load_gate(3, D - 1, 1)
 
         nc.vector.memset(bias_rows[:], 0.0)
         nc.scalar.dma_start(bias_rows[0:BLOCKS, :], b.rearrange("(c p) o -> c (p o)", p=P))
@@ -101,39 +112,44 @@ def tile_picked_sub_lin_relu2_sub_e_kernel(tc, xT, w, b, gate, offs, pos1, pos2,
                 in_=x_bf[a][:, lo:hi, :].rearrange("p s j -> p (s j)"),
             )
 
-        def interleave_w(copy, a, first, count, after=None):
-            w_bf[a, first] = sbuf(f"w_bf{a}{first}", [P, count * P, PACK], BF16, after)
-            cols = slice((first % 2) * P, (first % 2 + count) * P)
-            copy(w_bf[a, first][:], w_raw[a][first // 2][:, :, cols].rearrange("p j m -> p m j"))
+        def interleave_w(copy, a, c, after=None):
+            w_bf[a, c] = sbuf(f"w_bf{a}{c}", [P, P, PACK], BF16, after)
+            copy(w_bf[a, c][:], w_raw[a, c].rearrange("p j m -> p m j"))
 
-        def quantize_w(a, first, count, after=None):
-            codes = sbuf(f"w_codes{a}{first}", [P, count * P], U32, after)
-            scales = sbuf(f"w_scales{a}{first}", [P, count * P], U8)
-            nc.vector.quantize_mx(out=codes[:].bitcast(FP8X4), scales=scales[:], in_=w_bf[a, first][:].rearrange("p m j -> p (m j)"))
-            for i in range(count):
-                w_codes[a, first + i] = codes[:, i * P : (i + 1) * P]
-                w_scales[a, first + i] = scales[:, i * P : (i + 1) * P]
+        def quantize_w(a, c, after=None):
+            w_codes[a, c] = sbuf(f"w_codes{a}{c}", [P, P], U32, after)
+            w_scales[a, c] = sbuf(f"w_scales{a}{c}", [P, P], U8)
+            nc.vector.quantize_mx(
+                out=w_codes[a, c][:].bitcast(FP8X4), scales=w_scales[a, c][:], in_=w_bf[a, c][:].rearrange("p m j -> p (m j)")
+            )
 
         def product(acc, a, c, lo, hi):
             nc.tensor.matmul_mx(
                 out=acc,
-                lhsT=w_codes[a, c].bitcast(FP8X4),
-                lhsT_scale=w_scales[a, c],
+                lhsT=w_codes[a, c][:].bitcast(FP8X4),
+                lhsT_scale=w_scales[a, c][:],
                 rhs=x_codes[a][:, lo:hi].bitcast(FP8X4),
                 rhs_scale=x_scales[a][:, lo:hi],
                 start=(a == 0),
                 stop=(a == PASSES - 1),
             )
 
-        def activate(c):
-            relu = sbuf(f"relu{c}", [P, S], F32)
-            nc.scalar.activation(relu[:], z[c][:], ACT.Relu, bias=bias[:, c : c + 1])
-            nc.scalar.activation(y[c][:], relu[:], ACT.Square)
+        def activate(c, after=None):
+            relu = sbuf(f"relu{c}", [P, S], F32, after)
+            halves = [slice(u * HALF, (u + 1) * HALF) for u in range(2)]
+            for cols in halves:
+                nc.scalar.activation(relu[:, cols], z[c][:, cols], ACT.Relu, bias=bias[:, c : c + 1])
+            for cols in halves:
+                nc.scalar.activation(y[c][:, cols], relu[:, cols], ACT.Square)
 
-        def neighbour(c, d, after=None):
-            prod[c, d] = sbuf(f"prod{c}{d}", [P, V], F32, after)
-            weights = gate_first[d // 2][:, d % 2, :] if c == 0 else gate_sb[c][:, d, :]
-            nc.vector.tensor_tensor(prod[c, d][:], y[c][:].indirect(pos_sb[d][:]), weights, ALU.mult)
+        def neighbours(c, first, count, after=None):
+            tile = sbuf(f"prod{c}{first}", [P, count, V], F32, after)
+            for d in range(first, first + count):
+                prod[c, d] = tile[:, d - first, :]
+                neighbour(c, d)
+
+        def neighbour(c, d):
+            nc.vector.tensor_tensor(prod[c, d], y[c][:].indirect(pos_sb[d][:]), gate_sb[c, d], ALU.mult)
 
         def turn_and_add(acc, c, d, u, count):
             nc.tensor.matmul(
@@ -171,11 +187,11 @@ def tile_picked_sub_lin_relu2_sub_e_kernel(tc, xT, w, b, gate, offs, pos1, pos2,
 
         gather_x(0, 0, 0, S)
         gather_x(0, 1, 0, S)
-        for a in range(PASSES):
-            interleave_w(nc.scalar.copy, a, 0, 2)
+        for c in range(2):
+            interleave_w(nc.scalar.copy, 0, c)
         gather_x(0, 2, 0, S)
-        for a in range(PASSES):
-            quantize_w(a, 0, 2)
+        for c in range(2):
+            quantize_w(0, c)
         gather_x(0, 3, 0, S)
         quantize_x(0, 0, S)
         for u in range(2):
@@ -185,47 +201,47 @@ def tile_picked_sub_lin_relu2_sub_e_kernel(tc, xT, w, b, gate, offs, pos1, pos2,
             gather_x(1, j, 0, S)
         for u in range(2):
             gather_x(1, PACK - 1, u * HALF, (u + 1) * HALF)
+        for c in range(2):
+            interleave_w(nc.scalar.copy, 1, c)
+        quantize_x(1, 0, HALF)
+        quantize_w(1, 0)
+        quantize_x(1, HALF, S)
         for u in range(2):
-            quantize_x(1, u * HALF, (u + 1) * HALF)
             product(z_first[u][:], 1, 0, u * HALF, (u + 1) * HALF)
+        quantize_w(1, 1)
         product(z[1][:], 1, 1, 0, S)
         relu_first = [sbuf(f"relu_first{u}", [P, HALF], F32) for u in range(2)]
         for u in range(2):
             nc.scalar.activation(relu_first[u][:], z_first[u][:], ACT.Relu, bias=bias[:, 0:1])
-        for c in (2, 3):
-            interleave_w(nc.vector.tensor_copy, 0, c, 1)
-        for c in (2, 3):
-            quantize_w(0, c, 1)
+        interleave_w(nc.vector.tensor_copy, 0, 2)
         for u in range(2):
             nc.vector.tensor_tensor(y[0][:, u * HALF : (u + 1) * HALF], relu_first[u][:], relu_first[u][:], ALU.mult)
+        quantize_w(0, 2, after="relu_first0")
         product(z[2][:], 0, 2, 0, S)
-        product(z[3][:], 0, 3, 0, S)
         activate(1)
-        interleave_w(nc.scalar.copy, 1, 2, 1, after="relu_first0")
-        interleave_w(nc.scalar.copy, 1, 3, 1, after="relu_first1")
-        for d in range(2):
-            neighbour(0, d)
-        quantize_w(1, 2, 1, after="gate_first0")
+        interleave_w(nc.scalar.copy, 0, 3, after="relu_first1")
+        neighbours(0, 0, 2)
+        quantize_w(0, 3, after="gate00")
+        product(z[3][:], 0, 3, 0, S)
+        neighbours(0, 2, 2)
+        interleave_w(nc.scalar.copy, 1, 2)
+        quantize_w(1, 2)
         product(z[2][:], 1, 2, 0, S)
-        for d in range(2, D):
-            neighbour(0, d)
-        quantize_w(1, 3, 1, after="gate_first1")
+        interleave_w(nc.scalar.copy, 1, 3, after="relu_first1")
+        activate(2, after="w_raw13")
+        neighbours(1, 0, D - 1, after="w_bf12")
+        quantize_w(1, 3, after="gate10")
         product(z[3][:], 1, 3, 0, S)
-        activate(2)
-        neighbour(1, 0, after="relu_first0")
-        neighbour(1, 1)
-        neighbour(1, 2, after="relu_first1")
-        neighbour(1, 3)
-        activate(3)
+        neighbours(1, D - 1, 1, after="relu_first1")
+        activate(3, after="w_raw13")
         sum_whole(0, "z2")
         sum_whole(1, "z3")
         backs = {}
         for c, tags in ((2, ("pair0", "pair1")), (3, ("z1", "spare"))):
-            for d in range(D - 1):
-                neighbour(c, d)
+            neighbours(c, 0, D - 1)
             backs[c] = sum_part(c, tags)
+        neighbours(2, D - 1, 1, after="gate30")
+        neighbours(3, D - 1, 1)
         for c in (2, 3):
-            neighbour(c, D - 1)
-        for c in (2, 3):
-            nc.vector.tensor_tensor(result[c][:], prod[c, D - 1][:], backs[c][:], ALU.add)
+            nc.vector.tensor_tensor(result[c][:], prod[c, D - 1], backs[c][:], ALU.add)
             store(c)

from contextlib import ExitStack

import concourse.mybir as mybir
from concourse.masks import make_identity

K, T, D, S, V, N = 1024, 2048, 4, 512, 256, 512
FLOPS = 2 * K * N * S

F32 = mybir.dt.float32
BF16 = mybir.dt.bfloat16
U32 = mybir.dt.uint32
U16 = mybir.dt.uint16
U8 = mybir.dt.uint8
FP8X4 = mybir.dt.float8_e4m3fn_x4
ACT = mybir.ActivationFunctionType
ALU = mybir.AluOpType

P = 128
PACK = 4
K_PASS = P * PACK
PASSES = K // K_PASS
BLOCKS = N // P
HALF = S // 2
LIST_ROWS = 16


def tile_picked_sub_lin_relu2_sub_e_kernel(tc, xT, w, b, gate, offs, pos1, pos2, pos3, pos4, out):
    nc = tc.nc
    with ExitStack() as ctx:
        keep = ctx.enter_context(tc.tile_pool(name="keep", bufs=1))
        psum = ctx.enter_context(tc.psum_pool(name="psum", bufs=1))

        def sbuf(name, shape, dtype, after=None):
            return keep.tile(shape, dtype, name=name, tag=after or name, align_bytes=64)

        offs_sb = keep.tile([P, S // LIST_ROWS], U16, name="offs_sb")
        pos_sb = [keep.tile([P, V // LIST_ROWS], U16, name=f"pos_sb{d}") for d in range(D)]
        x_raw = [[sbuf(f"x_raw{a}{j}", [P, T], F32) for j in range(PACK)] for a in range(PASSES)]
        x_bf = [sbuf(f"x_bf{a}", [P, S, PACK], BF16) for a in range(PASSES)]
        x_codes = [sbuf(f"x_codes{a}", [P, S], U32) for a in range(PASSES)]
        x_scales = [sbuf(f"x_scales{a}", [P, S], U8) for a in range(PASSES)]
        y = [sbuf(f"y{c}", [P, S], F32) for c in range(BLOCKS)]
        result = [sbuf(f"result{c}", [P, V], F32) for c in range(BLOCKS)]
        ident = sbuf("ident", [P, P], F32)
        bias_rows = sbuf("bias_rows", [P, P], F32)
        bias = sbuf("bias", [P, BLOCKS], F32)
        warm = sbuf("warm", [P, 2], F32)
        w_raw, w_bf, w_codes, w_scales, gate_sb, prod = {}, {}, {}, {}, {}, {}

        z_first = [psum.tile([P, HALF], F32, name=f"z_first{u}", tag=f"pair{u}") for u in range(2)]
        z = [None] + [psum.tile([P, S], F32, name=f"z{c}", tag=f"z{c}") for c in range(1, BLOCKS)]

        x_rows = xT.rearrange("(a p j) t -> a j p t", a=PASSES, j=PACK)
        w_rows = w.rearrange("(a p j) m -> a p j m", a=PASSES, j=PACK)
        gate_rows = gate.rearrange("d (c p) v -> c p d v", p=P)

        def load_x(a, j):
            nc.sync.dma_start(x_raw[a][j][:], x_rows[a, j])

        def load_w(a, first, count):
            raw = sbuf(f"w_raw{a}{first}", [P, PACK, count * P], F32)
            nc.sync.dma_start(raw[:], w_rows[a, :, :, first * P : (first + count) * P])
            for i in range(count):
                w_raw[a, first + i] = raw[:, :, i * P : (i + 1) * P]

        def load_gate(c, first, count):
            tile = sbuf(f"gate{c}{first}", [P, count, V], F32)
            nc.sync.dma_start(tile[:], gate_rows[c, :, first : first + count, :])
            for i in range(count):
                gate_sb[c, first + i] = tile[:, i, :]

        load_x(0, 0)
        nc.sync.dma_start(offs_sb[:], offs)
        for d, pos in enumerate((pos1, pos2, pos3, pos4)):
            nc.sync.dma_start(pos_sb[d][:], pos)
        load_x(0, 1)
        load_w(0, 0, 2)
        load_x(0, 2)
        load_x(0, 3)
        for j in range(PACK):
            load_x(1, j)
        load_w(1, 0, 1)
        load_w(1, 1, 1)
        load_w(0, 2, 2)
        load_gate(0, 0, 2)
        load_gate(0, 2, 2)
        load_w(1, 2, 1)
        load_gate(1, 0, 2)
        load_w(1, 3, 1)
        load_gate(1, 2, 2)
        load_gate(2, 0, D)
        load_gate(3, 0, D - 1)
        load_gate(3, D - 1, 1)

        nc.vector.memset(bias_rows[:], 0.0)
        nc.scalar.dma_start(bias_rows[0:BLOCKS, :], b.rearrange("(c p) o -> c (p o)", p=P))
        make_identity(nc, ident[:])
        nc.scalar.activation(warm[:, 0:1], ident[:, 0:1], ACT.Relu)
        nc.scalar.activation(warm[:, 1:2], ident[:, 0:1], ACT.Square)
        bias_ps = psum.tile([P, P], F32, name="bias_ps", tag="back", bufs=2)
        nc.tensor.transpose(bias_ps[:], bias_rows[:], ident[:])
        nc.scalar.copy(bias[:], bias_ps[:, 0:BLOCKS])

        def gather_x(a, j, lo, hi):
            window = x_raw[a][j][:].indirect(offs_sb[:, lo // LIST_ROWS : hi // LIST_ROWS])
            nc.vector.tensor_copy(x_bf[a][:, lo:hi, j], window)

        def quantize_x(a, lo, hi):
            nc.vector.quantize_mx(
                out=x_codes[a][:, lo:hi].bitcast(FP8X4),
                scales=x_scales[a][:, lo:hi],
                in_=x_bf[a][:, lo:hi, :].rearrange("p s j -> p (s j)"),
            )

        def interleave_w(copy, a, c, after=None):
            w_bf[a, c] = sbuf(f"w_bf{a}{c}", [P, P, PACK], BF16, after)
            copy(w_bf[a, c][:], w_raw[a, c].rearrange("p j m -> p m j"))

        def quantize_w(a, c, after=None):
            w_codes[a, c] = sbuf(f"w_codes{a}{c}", [P, P], U32, after)
            w_scales[a, c] = sbuf(f"w_scales{a}{c}", [P, P], U8)
            nc.vector.quantize_mx(
                out=w_codes[a, c][:].bitcast(FP8X4), scales=w_scales[a, c][:], in_=w_bf[a, c][:].rearrange("p m j -> p (m j)")
            )

        def product(acc, a, c, lo, hi):
            nc.tensor.matmul_mx(
                out=acc,
                lhsT=w_codes[a, c][:].bitcast(FP8X4),
                lhsT_scale=w_scales[a, c][:],
                rhs=x_codes[a][:, lo:hi].bitcast(FP8X4),
                rhs_scale=x_scales[a][:, lo:hi],
                start=(a == 0),
                stop=(a == PASSES - 1),
            )

        def activate(c, after=None):
            relu = sbuf(f"relu{c}", [P, S], F32, after)
            halves = [slice(u * HALF, (u + 1) * HALF) for u in range(2)]
            for cols in halves:
                nc.scalar.activation(relu[:, cols], z[c][:, cols], ACT.Relu, bias=bias[:, c : c + 1])
            for cols in halves:
                nc.scalar.activation(y[c][:, cols], relu[:, cols], ACT.Square)

        def neighbours(c, first, count, after=None):
            tile = sbuf(f"prod{c}{first}", [P, count, V], F32, after)
            for d in range(first, first + count):
                prod[c, d] = tile[:, d - first, :]
                neighbour(c, d)

        def neighbour(c, d):
            nc.vector.tensor_tensor(prod[c, d], y[c][:].indirect(pos_sb[d][:]), gate_sb[c, d], ALU.mult)

        def turn_and_add(acc, c, d, u, count):
            nc.tensor.matmul(
                acc, prod[c, d][:, u * P : (u + 1) * P], ident[:], start=(d == 0), stop=(d == count - 1), is_transpose=True
            )

        def turn_back(c, turned_sb):
            back = psum.tile([P, V], F32, name=f"back{c}", tag="back", bufs=2)
            for u in range(2):
                nc.tensor.transpose(back[:, u * P : (u + 1) * P], turned_sb[:, u, :], ident[:])
            return back

        def store(c):
            nc.sync.dma_start(out[c * P : (c + 1) * P, :], result[c][:])

        def sum_whole(c, tag):
            turned = psum.tile([P, 2, P], F32, name=f"turned{c}", tag=tag)
            for u in range(2):
                for d in range(D):
                    turn_and_add(turned[:, u, :], c, d, u, D)
            turned_sb = sbuf(f"turned_sb{c}", [P, 2, P], F32)
            nc.scalar.copy(turned_sb[:], turned[:])
            nc.scalar.copy(result[c][:], turn_back(c, turned_sb)[:])
            store(c)

        def sum_part(c, tags):
            turned = [psum.tile([P, P], F32, name=f"turned{c}{u}", tag=tags[u]) for u in range(2)]
            for d in range(D - 1):
                for u in range(2):
                    turn_and_add(turned[u][:], c, d, u, D - 1)
            turned_sb = sbuf(f"turned_sb{c}", [P, 2, P], F32)
            for u in range(2):
                nc.scalar.copy(turned_sb[:, u, :], turned[u][:])
            return turn_back(c, turned_sb)

        gather_x(0, 0, 0, S)
        gather_x(0, 1, 0, S)
        for c in range(2):
            interleave_w(nc.scalar.copy, 0, c)
        gather_x(0, 2, 0, S)
        for c in range(2):
            quantize_w(0, c)
        gather_x(0, 3, 0, S)
        quantize_x(0, 0, S)
        for u in range(2):
            product(z_first[u][:], 0, 0, u * HALF, (u + 1) * HALF)
        product(z[1][:], 0, 1, 0, S)
        for j in range(PACK - 1):
            gather_x(1, j, 0, S)
        for u in range(2):
            gather_x(1, PACK - 1, u * HALF, (u + 1) * HALF)
        for c in range(2):
            interleave_w(nc.scalar.copy, 1, c)
        quantize_x(1, 0, HALF)
        quantize_w(1, 0)
        quantize_x(1, HALF, S)
        for u in range(2):
            product(z_first[u][:], 1, 0, u * HALF, (u + 1) * HALF)
        quantize_w(1, 1)
        product(z[1][:], 1, 1, 0, S)
        relu_first = [sbuf(f"relu_first{u}", [P, HALF], F32) for u in range(2)]
        for u in range(2):
            nc.scalar.activation(relu_first[u][:], z_first[u][:], ACT.Relu, bias=bias[:, 0:1])
        interleave_w(nc.vector.tensor_copy, 0, 2)
        for u in range(2):
            nc.vector.tensor_tensor(y[0][:, u * HALF : (u + 1) * HALF], relu_first[u][:], relu_first[u][:], ALU.mult)
        quantize_w(0, 2, after="relu_first0")
        product(z[2][:], 0, 2, 0, S)
        activate(1)
        interleave_w(nc.scalar.copy, 0, 3, after="relu_first1")
        neighbours(0, 0, 2)
        quantize_w(0, 3, after="gate00")
        product(z[3][:], 0, 3, 0, S)
        neighbours(0, 2, 2)
        interleave_w(nc.scalar.copy, 1, 2)
        quantize_w(1, 2)
        product(z[2][:], 1, 2, 0, S)
        interleave_w(nc.scalar.copy, 1, 3, after="relu_first1")
        activate(2, after="w_raw13")
        neighbours(1, 0, D - 1, after="w_bf12")
        quantize_w(1, 3, after="gate10")
        product(z[3][:], 1, 3, 0, S)
        neighbours(1, D - 1, 1, after="relu_first1")
        activate(3, after="w_raw13")
        sum_whole(0, "z2")
        sum_whole(1, "z3")
        backs = {}
        for c, tags in ((2, ("pair0", "pair1")), (3, ("z1", "spare"))):
            neighbours(c, 0, D - 1)
            backs[c] = sum_part(c, tags)
        neighbours(2, D - 1, 1, after="gate30")
        neighbours(3, D - 1, 1)
        for c in (2, 3):
            nc.vector.tensor_tensor(result[c][:], prod[c, D - 1], backs[c][:], ALU.add)
            store(c)
